import numpy as np
import ml_dtypes


def mxq(x, axis, fmt="e4m3"):
    dtype, down = {"e4m3": (ml_dtypes.float8_e4m3fn, 7), "e5m2": (ml_dtypes.float8_e5m2, 14)}[fmt]
    v = np.moveaxis(np.asarray(x, np.float32).astype(ml_dtypes.bfloat16).astype(np.float64), axis, -1)
    blocks = v.reshape(v.shape[:-1] + (-1, 32))
    amax = np.abs(blocks).max(-1, keepdims=True)
    byte = np.maximum(np.where(amax > 0, np.frexp(amax)[1] - 1 + 127, 0) - down, 1)
    scale = np.exp2(byte - 127.0)
    codes = (blocks / scale).astype(np.float32).astype(dtype).astype(np.float64)
    return np.moveaxis((codes * scale).reshape(v.shape), -1, axis)


WIDE = False


def mx_kscale(k, group=512):
    if not WIDE:
        return np.ones(k)
    levels = np.array([18, -18])
    if group != 512:
        return np.exp2(np.random.permutation(np.resize(levels, k // group))).repeat(group)
    if k % 512:
        return np.exp2(np.random.permutation(np.resize(levels, k // 32))).repeat(32)
    a = np.empty((k // 512, 16))
    for p in range(k // 512):
        a[p, :8] = np.random.permutation(np.resize(levels, 8))
        for g in range(8):
            far = levels[np.abs(levels - a[p, g]) >= 10]
            a[p, g + 8] = far[np.random.randint(len(far))]
    return np.exp2(a.ravel()).repeat(32)


def f64(x):
    return np.asarray(x).astype(np.float64)


G, D, I, F, E = 8, 128, 128, 128, 128


def sgn(shape):
    return np.random.uniform(0.5, 2.0, shape) * np.where(np.random.standard_normal(shape) < 0, -1.0, 1.0)


def setup_inputs():
    n = np.random.standard_normal
    s_d = mx_kscale(D, 0)
    s_i = mx_kscale(I, 0)
    return {
        "kT": (n((G, D, I)) / np.sqrt(D) / s_d[:, None]).astype(np.float32),
        "S": (n((G, D, E)) * s_d[:, None]).astype(np.float32),
        "v": (n((G, I, E))).astype(np.float32),
        "be": (sgn((G, I, 1)) * s_i[:, None]).astype(np.float32),
        "kn": (n((G, I, F)) / np.sqrt(I) / s_i[:, None] * s_d).astype(np.float32),
        "mo": (n((G, F, E)) * s_d[:, None]).astype(np.float32),
    }


def reference(kT, S, v, be, kn, mo):
    kTq = mxq(f64(kT), 1, "e4m3")
    Sq = mxq(f64(S), 1, "e4m3")
    z = kTq.transpose(0, 2, 1) @ Sq
    u = (f64(v) - z) * f64(be)
    knq = mxq(f64(kn), 1, "e4m3")
    uq = mxq(u, 1, "e4m3")
    w = knq.transpose(0, 2, 1) @ uq
    o = 0.95 * f64(S) + 0.9 * f64(mo) + w
    return o

@@ -1,0 +1,228 @@
+from contextlib import ExitStack
+
+import concourse.mybir as mybir
+
+G, D = 8, 128
+FLOPS = 2 * 2 * G * D * D * D
+
+F32 = mybir.dt.float32
+BF16 = mybir.dt.bfloat16
+U32 = mybir.dt.uint32
+I32 = mybir.dt.int32
+U8 = mybir.dt.uint8
+FP8X4 = mybir.dt.float8_e4m3fn_x4
+ALU = mybir.AluOpType
+ACT = mybir.ActivationFunctionType
+
+P = 128
+R = 32
+PACK = 4
+FIRST_HEAD = (0, 4, 2, 6)
+
+
+def tile_rows_upd_titans_kernel(tc, kT, S, v, be, kn, mo, out):
+    nc = tc.nc
+    with ExitStack() as ctx:
+        sb = ctx.enter_context(tc.tile_pool(name="sb", bufs=1))
+        ps = ctx.enter_context(tc.psum_pool(name="ps", bufs=1))
+        ctx.enter_context(tc.manual_schedule())
+
+        def pair(name, shape, dtype):
+            return [sb.tile(shape, dtype, name=f"{name}{i}", align_bytes=64) for i in range(2)]
+
+        k_raw = pair("k_raw", [P, PACK, D], F32)
+        s_raw = pair("s_raw", [P, PACK, D], F32)
+        k_bf = pair("k_bf", [P, PACK, 2, R, PACK], BF16)
+        s_bf = pair("s_bf", [P, D, PACK], BF16)
+        codes1 = sb.tile([P, 6 * D], U32, name="codes1", align_bytes=64)
+        scales1 = sb.tile([P, 6 * D], U8, name="scales1", align_bytes=64)
+        v_raw = sb.tile([P, 2, PACK, D], F32, name="v_raw")
+        n_raw = sb.tile([P, 2, PACK, D], F32, name="n_raw")
+        be_sb = sb.tile([P, 2, 8], F32, name="be_sb")
+        vb = pair("vb", [P, PACK, D], F32)
+        zb = pair("zb", [P, PACK, D], F32)
+        u_bf = pair("u_bf", [P, D, PACK], BF16)
+        n_bf = pair("n_bf", [P, D, PACK], BF16)
+        u_codes = pair("u_codes", [P, D], U32)
+        u_scales = pair("u_scales", [P, D], U8)
+        n_codes = pair("n_codes", [P, D], U32)
+        n_scales = pair("n_scales", [P, D], U8)
+        s_nat = pair("s_nat", [P, 4, D], F32)
+        m_nat = pair("m_nat", [P, 4, D], F32)
+        acc = pair("acc", [P, 4, D], F32)
+        res = pair("res", [P, 4, D], F32)
+        warm = sb.tile([P, 8], F32, name="warm")
+        warm_out = sb.tile([P, 8], F32, name="warm_out")
+        bank = [[ps.tile([P, 4, D], F32, name=f"bank{r}_{h}") for h in range(2)] for r in range(4)]
+
+        S_AT = (5 * D, 0)
+        K_AT = (D, 3 * D)
+
+        def load_rows(eng, dst, src, ab):
+            eng.dma_start(out=dst[ab][:], in_=src[4 * ab : 4 * ab + 4].rearrange("g (p t) c -> (g p) t c", t=PACK))
+
+        def load_quad(eng, dst, src, q):
+            h = FIRST_HEAD[q]
+            eng.dma_start(
+                out=dst[R * q : R * q + R].rearrange("p s t c -> p s (t c)"),
+                in_=src[h : h + 2].rearrange("s (p t) c -> p s (t c)", t=PACK),
+            )
+
+        def nat(src, s):
+            return src.rearrange("(k s) f e -> s f k e", s=2)[s]
+
+        def interleave(copy, dst, src):
+            copy(out=dst.rearrange("p (c i) t -> p c t i", i=4), in_=src.rearrange("p t (c i) -> p c t i", i=4))
+
+        def deal_keys(ab):
+            nc.scalar.copy(
+                out=k_bf[ab][:, :, ab, :, :].rearrange("p j m t -> p m t j"),
+                in_=k_raw[ab][:].rearrange("p t (m j) -> p m t j", j=PACK),
+            )
+
+        def quantize(codes, scales, src):
+            nc.vector.quantize_mx(out=codes.bitcast(FP8X4), scales=scales, in_=src)
+
+        def quantize_keys(ab):
+            cols = slice(K_AT[ab], K_AT[ab] + 2 * D)
+            quantize(codes1[:, cols], scales1[:, cols], k_bf[ab][:].rearrange("p j z m t -> p (j z m t)"))
+
+        def quantize_state(ab):
+            cols = slice(S_AT[ab], S_AT[ab] + D)
+            quantize(codes1[:, cols], scales1[:, cols], s_bf[ab][:].rearrange("p c t -> p (c t)"))
+
+        def useful(r):
+            return slice(64 * (r // 2), 64 * (r // 2) + 64)
+
+        def scale_z_scalar(r, h):
+            rows = useful(r)
+            for jj in range(2):
+                j = 2 * h + jj
+                nc.scalar.activation(
+                    out=zb[r % 2][rows, j, :], in_=bank[r][h][rows, jj, :], func=ACT.Copy, scale=be_sb[rows, r % 2, j : j + 1]
+                )
+
+        def scale_z_vector(r, h):
+            rows = useful(r)
+            nc.vector.tensor_tensor(
+                out=zb[r % 2][rows, 2 * h : 2 * h + 2, :],
+                in0=bank[r][h][rows, 0:2, :],
+                in1=be_sb[rows, r % 2, 2 * h : 2 * h + 2].unsqueeze(2).to_broadcast([64, 2, D]),
+                op=ALU.mult,
+            )
+
+        def make_u(s):
+            nc.vector.tensor_tensor(
+                out=u_bf[s][:].rearrange("p (c i) j -> p c j i", i=4),
+                in0=vb[s][:].rearrange("p j (c i) -> p c j i", i=4),
+                in1=zb[s][:].rearrange("p j (c i) -> p c j i", i=4),
+                op=ALU.subtract,
+            )
+
+        def second_product(s):
+            for q in range(4):
+                rows = slice(R * q, R * q + R)
+                nc.tensor.matmul_mx(
+                    out=bank[q][s][:, 2, :],
+                    lhsT=n_codes[s][rows, :].bitcast(FP8X4),
+                    lhsT_scale=n_scales[s][rows, :],
+                    rhs=u_codes[s][rows, :].bitcast(FP8X4),
+                    rhs_scale=u_scales[s][rows, :],
+                    start=True,
+                    stop=True,
+                )
+
+        def add_state(s):
+            for q in (0, 2, 1, 3):
+                k = FIRST_HEAD[q] // 2
+                nc.vector.scalar_tensor_tensor(
+                    out=acc[s][:, k, :], in0=s_nat[s][:, k, :], scalar=0.95, in1=bank[q][s][:, 2, :], op0=ALU.mult, op1=ALU.add
+                )
+
+        def add_momentum(s, ks):
+            nc.vector.scalar_tensor_tensor(
+                out=res[s][:, ks, :], in0=m_nat[s][:, ks, :], scalar=0.9, in1=acc[s][:, ks, :], op0=ALU.mult, op1=ALU.add
+            )
+
+        for ab in range(2):
+            load_rows(nc.sync, k_raw, kT, ab)
+        for ab in range(2):
+            load_rows(nc.sync, s_raw, S, ab)
+        for q in range(4):
+            h = FIRST_HEAD[q]
+            nc.scalar.dma_start(
+                out=be_sb[R * q : R * q + R, :, 0:PACK], in_=be[h : h + 2].rearrange("s (p j) o -> p s (j o)", j=PACK)
+            )
+        for q in range(2):
+            load_quad(nc.sync, v_raw, v, q)
+        for q in range(2):
+            load_quad(nc.sync, n_raw, kn, q)
+
+        nc.vector.memset(warm[:], 0.0)
+        nc.scalar.activation(out=warm_out[:], in_=warm[:], func=ACT.Copy, scale=warm[:, 0:1])
+        for ab in range(2):
+            nc.vector.memset(k_bf[ab][:].rearrange("p j z m t -> p (j z m t)").bitcast(I32), 0)
+
+        deal_keys(0)
+        for q in range(2, 4):
+            load_quad(nc.scalar, v_raw, v, q)
+        deal_keys(1)
+        for q in range(2, 4):
+            load_quad(nc.scalar, n_raw, kn, q)
+        for s in range(2):
+            nc.sync.dma_start(out=s_nat[s][:], in_=nat(S, s))
+            nc.sync.dma_start(out=m_nat[s][:], in_=nat(mo, s))
+
+        quantize_keys(0)
+        interleave(nc.vector.tensor_copy, s_bf[0][:], s_raw[0][:])
+        quantize_keys(1)
+        interleave(nc.vector.tensor_copy, s_bf[1][:], s_raw[1][:])
+        quantize_state(0)
+        quantize_state(1)
+
+        for s in range(2):
+            for j in range(PACK):
+                nc.gpsimd.tensor_scalar(
+                    out=vb[s][:, j, :], in0=v_raw[:, s, j, :], scalar1=be_sb[:, s, j : j + 1], scalar2=0.0, op0=ALU.mult, op1=ALU.add
+                )
+
+        for j in range(PACK):
+            for ab in range(2):
+                for r in range(4):
+                    rows = slice(R * r, R * r + R)
+                    c0 = K_AT[ab] + 64 * j - 64 * (r // 2)
+                    nc.tensor.matmul_mx(
+                        out=bank[r][j // 2][:, j % 2, :],
+                        lhsT=codes1[rows, c0 : c0 + D].bitcast(FP8X4),
+                        lhsT_scale=scales1[rows, c0 : c0 + D],
+                        rhs=codes1[rows, S_AT[ab] : S_AT[ab] + D].bitcast(FP8X4),
+                        rhs_scale=scales1[rows, S_AT[ab] : S_AT[ab] + D],
+                        start=(ab == 0),
+                        stop=(ab == 1),
+                    )
+
+        scale_z_scalar(0, 0)
+        scale_z_vector(2, 0)
+        scale_z_scalar(1, 0)
+        scale_z_vector(3, 0)
+        scale_z_scalar(0, 1)
+        scale_z_vector(2, 1)
+        scale_z_scalar(1, 1)
+        scale_z_scalar(3, 1)
+        make_u(0)
+        make_u(1)
+        for s in range(2):
+            interleave(nc.scalar.copy, n_bf[s][:], n_raw[:, s])
+        for s in range(2):
+            quantize(u_codes[s][:], u_scales[s][:], u_bf[s][:].rearrange("p c t -> p (c t)"))
+        for s in range(2):
+            quantize(n_codes[s][:], n_scales[s][:], n_bf[s][:].rearrange("p c t -> p (c t)"))
+            second_product(s)
+        add_state(0)
+        add_momentum(0, slice(0, 4))
+        nc.sync.dma_start(out=nat(out, 0), in_=res[0][:])
+        add_state(1)
+        for half in range(2):
+            ks = slice(2 * half, 2 * half + 2)
+            add_momentum(1, ks)
+            nc.sync.dma_start(out=nat(out, 1)[:, ks, :], in_=res[1][:, ks, :])

@@ -53,9 +53,26 @@ def tile_rows_upd_titans_kernel(tc, kT, S, v, be, kn, mo, out):
         res = pair("res", [P, 4, D], F32)
         warm = sb.tile([P, 8], F32, name="warm")
         warm_out = sb.tile([P, 8], F32, name="warm_out")
-        bank = [[ps.tile([P, 4, D], F32, name=f"bank{r}_{h}") for h in range(2)] for r in range(4)]
+        z_codes = sb.tile([P, D], U32, name="z_codes", align_bytes=64)
+        z_scales = sb.tile([P, D], U8, name="z_scales", align_bytes=64)
+        banks = [ps.tile([P, 4, D], F32, name=f"bank{i}") for i in range(8)]
+        bank = [[banks[0], banks[1]], [banks[2], banks[3]], [banks[4], banks[4]], [banks[5], banks[6]]]
+        warm_bank = banks[7]
 
-        S_AT = (5 * D, 0)
+        def warm_up(codes, scales, n):
+            for i in range(n):
+                nc.tensor.matmul_mx(
+                    out=warm_bank[:, i % 4, :],
+                    lhsT=codes.bitcast(FP8X4),
+                    lhsT_scale=scales,
+                    rhs=codes.bitcast(FP8X4),
+                    rhs_scale=scales,
+                    start=True,
+                    stop=True,
+                )
+
+
+        S_AT = (0, 5 * D)
         K_AT = (D, 3 * D)
 
         def load_rows(eng, dst, src, ab):
@@ -76,8 +93,8 @@ def tile_rows_upd_titans_kernel(tc, kT, S, v, be, kn, mo, out):
 
         def deal_keys(ab):
             nc.scalar.copy(
-                out=k_bf[ab][:, :, ab, :, :].rearrange("p j m t -> p m t j"),
-                in_=k_raw[ab][:].rearrange("p t (m j) -> p m t j", j=PACK),
+                out=k_bf[ab][:, :, ab, :, :].rearrange("p j m t -> p m j t"),
+                in_=k_raw[ab][:].rearrange("p t (m j) -> p m j t", j=PACK),
             )
 
         def quantize(codes, scales, src):
@@ -99,15 +116,15 @@ def tile_rows_upd_titans_kernel(tc, kT, S, v, be, kn, mo, out):
             for jj in range(2):
                 j = 2 * h + jj
                 nc.scalar.activation(
-                    out=zb[r % 2][rows, j, :], in_=bank[r][h][rows, jj, :], func=ACT.Copy, scale=be_sb[rows, r % 2, j : j + 1]
+                    out=zb[r % 2][rows, j, :], in_=bank[r][h][rows, j, :], func=ACT.Copy, scale=be_sb[rows, r % 2, j : j + 1]
                 )
 
-        def scale_z_vector(r, h):
+        def scale_z_vector(r, j0, j1):
             rows = useful(r)
             nc.vector.tensor_tensor(
-                out=zb[r % 2][rows, 2 * h : 2 * h + 2, :],
-                in0=bank[r][h][rows, 0:2, :],
-                in1=be_sb[rows, r % 2, 2 * h : 2 * h + 2].unsqueeze(2).to_broadcast([64, 2, D]),
+                out=zb[r % 2][rows, j0:j1, :],
+                in0=bank[r][j0 // 2][rows, j0:j1, :],
+                in1=be_sb[rows, r % 2, j0:j1].unsqueeze(2).to_broadcast([64, j1 - j0, D]),
                 op=ALU.mult,
             )
 
@@ -120,10 +137,10 @@ def tile_rows_upd_titans_kernel(tc, kT, S, v, be, kn, mo, out):
             )
 
         def second_product(s):
-            for q in range(4):
+            for q in ((2, 0, 1, 3), (1, 3, 0, 2))[s]:
                 rows = slice(R * q, R * q + R)
                 nc.tensor.matmul_mx(
-                    out=bank[q][s][:, 2, :],
+                    out=bank[q][s][:, s, :],
                     lhsT=n_codes[s][rows, :].bitcast(FP8X4),
                     lhsT_scale=n_scales[s][rows, :],
                     rhs=u_codes[s][rows, :].bitcast(FP8X4),
@@ -132,97 +149,130 @@ def tile_rows_upd_titans_kernel(tc, kT, S, v, be, kn, mo, out):
                     stop=True,
                 )
 
-        def add_state(s):
-            for q in (0, 2, 1, 3):
+        def make_base(s, half):
+            ks = slice(2 * half, 2 * half + 2)
+            nc.vector.scalar_tensor_tensor(
+                out=acc[s][:, ks, :], in0=s_nat[s][:, ks, :], scalar=0.95 / 0.9, in1=m_nat[s][:, ks, :], op0=ALU.mult, op1=ALU.add
+            )
+
+        def finish(s, qs):
+            for q in qs:
                 k = FIRST_HEAD[q] // 2
                 nc.vector.scalar_tensor_tensor(
-                    out=acc[s][:, k, :], in0=s_nat[s][:, k, :], scalar=0.95, in1=bank[q][s][:, 2, :], op0=ALU.mult, op1=ALU.add
+                    out=res[s][:, k, :], in0=acc[s][:, k, :], scalar=0.9, in1=bank[q][s][:, s, :], op0=ALU.mult, op1=ALU.add
                 )
 
-        def add_momentum(s, ks):
-            nc.vector.scalar_tensor_tensor(
-                out=res[s][:, ks, :], in0=m_nat[s][:, ks, :], scalar=0.9, in1=acc[s][:, ks, :], op0=ALU.mult, op1=ALU.add
+        def store(eng, s, k0, k1):
+            eng.dma_start(out=nat(out, s)[:, k0:k1, :], in_=res[s][:, k0:k1, :])
+
+        def scale_v_scalar(s):
+            for j in range(PACK):
+                nc.scalar.activation(out=vb[s][:, j, :], in_=v_raw[:, s, j, :], func=ACT.Copy, scale=be_sb[:, s, j : j + 1])
+
+        def load_steps(eng, q):
+            h = FIRST_HEAD[q]
+            eng.dma_start(out=be_sb[R * q : R * q + R, :, 0:PACK], in_=be[h : h + 2].rearrange("s (p j) o -> p s (j o)", j=PACK))
+
+        def z_pass(r, j, ab):
+            rows = slice(R * r, R * r + R)
+            c0 = K_AT[ab] + 64 * j - 64 * (r // 2)
+            nc.tensor.matmul_mx(
+                out=bank[r][j // 2][:, j, :],
+                lhsT=codes1[rows, c0 : c0 + D].bitcast(FP8X4),
+                lhsT_scale=scales1[rows, c0 : c0 + D],
+                rhs=codes1[rows, S_AT[ab] : S_AT[ab] + D].bitcast(FP8X4),
+                rhs_scale=scales1[rows, S_AT[ab] : S_AT[ab] + D],
+                start=(ab == 0),
+                stop=(ab == 1),
             )
 
-        for ab in range(2):
-            load_rows(nc.sync, k_raw, kT, ab)
-        for ab in range(2):
-            load_rows(nc.sync, s_raw, S, ab)
-        for q in range(4):
-            h = FIRST_HEAD[q]
-            nc.scalar.dma_start(
-                out=be_sb[R * q : R * q + R, :, 0:PACK], in_=be[h : h + 2].rearrange("s (p j) o -> p s (j o)", j=PACK)
-            )
+        early = [(0, 0), (2, 0), (0, 2), (1, 0), (3, 0), (1, 2), (3, 2)]
+
+        def first_product(tiles):
+            for j in range(PACK):
+                for ab in range(2):
+                    for r in tiles:
+                        if ab == 1 or (r, j) not in early:
+                            z_pass(r, j, ab)
+
+        def scale_v(s):
+            for j in range(PACK):
+                nc.vector.tensor_scalar(
+                    out=vb[s][:, j, :], in0=v_raw[:, s, j, :], scalar1=be_sb[:, s, j : j + 1], scalar2=None, op0=ALU.mult
+                )
+
+        def flat(t):
+            return t[:].rearrange("p c t -> p (c t)")
+
+        load_rows(nc.sync, k_raw, kT, 0)
         for q in range(2):
-            load_quad(nc.sync, v_raw, v, q)
-        for q in range(2):
-            load_quad(nc.sync, n_raw, kn, q)
+            load_steps(nc.gpsimd, q)
+            load_steps(nc.scalar, q + 2)
+        load_rows(nc.sync, s_raw, S, 0)
+        load_rows(nc.sync, k_raw, kT, 1)
+        load_rows(nc.sync, s_raw, S, 1)
+        for dst, src in ((n_raw, kn), (v_raw, v)):
+            for q in (0, 2, 1, 3):
+                load_quad(nc.sync, dst, src, q)
+        for s in range(2):
+            nc.sync.dma_start(out=s_nat[s][:], in_=nat(S, s))
+            nc.sync.dma_start(out=m_nat[s][:], in_=nat(mo, s))
 
         nc.vector.memset(warm[:], 0.0)
         nc.scalar.activation(out=warm_out[:], in_=warm[:], func=ACT.Copy, scale=warm[:, 0:1])
         for ab in range(2):
             nc.vector.memset(k_bf[ab][:].rearrange("p j z m t -> p (j z m t)").bitcast(I32), 0)
+        quantize(z_codes[:], z_scales[:], k_bf[0][:, 0:2].rearrange("p j z m t -> p (j z m t)"))
+        warm_up(z_codes[:], z_scales[:], 24)
 
         deal_keys(0)
-        for q in range(2, 4):
-            load_quad(nc.scalar, v_raw, v, q)
-        deal_keys(1)
-        for q in range(2, 4):
-            load_quad(nc.scalar, n_raw, kn, q)
-        for s in range(2):
-            nc.sync.dma_start(out=s_nat[s][:], in_=nat(S, s))
-            nc.sync.dma_start(out=m_nat[s][:], in_=nat(mo, s))
-
-        quantize_keys(0)
         interleave(nc.vector.tensor_copy, s_bf[0][:], s_raw[0][:])
-        quantize_keys(1)
-        interleave(nc.vector.tensor_copy, s_bf[1][:], s_raw[1][:])
+        quantize_keys(0)
+        warm_up(codes1[:, D : 2 * D], scales1[:, D : 2 * D], 4)
         quantize_state(0)
+        warm_up(codes1[:, 0:D], scales1[:, 0:D], 2)
+        deal_keys(1)
+        interleave(nc.vector.tensor_copy, s_bf[1][:], s_raw[1][:])
+        quantize_keys(1)
+        for r, j in early:
+            z_pass(r, j, 0)
         quantize_state(1)
+        first_product((0, 2))
+        first_product((1, 3))
+        warm_up(z_codes[:], z_scales[:], 18)
 
-        for s in range(2):
-            for j in range(PACK):
-                nc.gpsimd.tensor_scalar(
-                    out=vb[s][:, j, :], in0=v_raw[:, s, j, :], scalar1=be_sb[:, s, j : j + 1], scalar2=0.0, op0=ALU.mult, op1=ALU.add
-                )
-
-        for j in range(PACK):
-            for ab in range(2):
-                for r in range(4):
-                    rows = slice(R * r, R * r + R)
-                    c0 = K_AT[ab] + 64 * j - 64 * (r // 2)
-                    nc.tensor.matmul_mx(
-                        out=bank[r][j // 2][:, j % 2, :],
-                        lhsT=codes1[rows, c0 : c0 + D].bitcast(FP8X4),
-                        lhsT_scale=scales1[rows, c0 : c0 + D],
-                        rhs=codes1[rows, S_AT[ab] : S_AT[ab] + D].bitcast(FP8X4),
-                        rhs_scale=scales1[rows, S_AT[ab] : S_AT[ab] + D],
-                        start=(ab == 0),
-                        stop=(ab == 1),
-                    )
+        interleave(nc.scalar.copy, n_bf[0][:], n_raw[:, 0])
+        interleave(nc.vector.tensor_copy, n_bf[1][:], n_raw[:, 1])
+        quantize(n_codes[1][:], n_scales[1][:], flat(n_bf[1]))
+        quantize(n_codes[0][:], n_scales[0][:], flat(n_bf[0]))
 
         scale_z_scalar(0, 0)
-        scale_z_vector(2, 0)
-        scale_z_scalar(1, 0)
-        scale_z_vector(3, 0)
         scale_z_scalar(0, 1)
-        scale_z_vector(2, 1)
+        scale_z_vector(2, 0, 4)
+        scale_v(0)
+        scale_v(1)
+        scale_z_scalar(1, 0)
+        scale_z_scalar(3, 0)
+        make_u(0)
         scale_z_scalar(1, 1)
         scale_z_scalar(3, 1)
-        make_u(0)
+        make_base(0, 0)
+        quantize(u_codes[0][:], u_scales[0][:], flat(u_bf[0]))
         make_u(1)
-        for s in range(2):
-            interleave(nc.scalar.copy, n_bf[s][:], n_raw[:, s])
-        for s in range(2):
-            quantize(u_codes[s][:], u_scales[s][:], u_bf[s][:].rearrange("p c t -> p (c t)"))
-        for s in range(2):
-            quantize(n_codes[s][:], n_scales[s][:], n_bf[s][:].rearrange("p c t -> p (c t)"))
-            second_product(s)
-        add_state(0)
-        add_momentum(0, slice(0, 4))
-        nc.sync.dma_start(out=nat(out, 0), in_=res[0][:])
-        add_state(1)
-        for half in range(2):
-            ks = slice(2 * half, 2 * half + 2)
-            add_momentum(1, ks)
-            nc.sync.dma_start(out=nat(out, 1)[:, ks, :], in_=res[1][:, ks, :])
+        second_product(0)
+        make_base(0, 1)
+        quantize(u_codes[1][:], u_scales[1][:], flat(u_bf[1]))
+        finish(0, (2,))
+        second_product(1)
+        finish(0, (0,))
+        store(nc.sync, 0, 0, 2)
+        finish(0, (1, 3))
+        store(nc.sync, 0, 2, 4)
+        make_base(1, 1)
+        make_base(1, 0)
+        finish(1, (1, 3))
+        store(nc.sync, 1, 2, 4)
+        finish(1, (0,))
+        store(nc.scalar, 1, 0, 1)
+        finish(1, (2,))
+        store(nc.sync, 1, 1, 2)

@@ -205,9 +205,8 @@ def tile_rows_upd_titans_kernel(tc, kT, S, v, be, kn, mo, out):
             return t[:].rearrange("p c t -> p (c t)")
 
         load_rows(nc.sync, k_raw, kT, 0)
-        for q in range(2):
-            load_steps(nc.gpsimd, q)
-            load_steps(nc.scalar, q + 2)
+        for q in range(4):
+            load_steps(nc.scalar, q)
         load_rows(nc.sync, s_raw, S, 0)
         load_rows(nc.sync, k_raw, kT, 1)
         load_rows(nc.sync, s_raw, S, 1)
@@ -220,17 +219,18 @@ def tile_rows_upd_titans_kernel(tc, kT, S, v, be, kn, mo, out):
 
         nc.vector.memset(warm[:], 0.0)
         nc.scalar.activation(out=warm_out[:], in_=warm[:], func=ACT.Copy, scale=warm[:, 0:1])
+        nc.vector.memset(flat(u_bf[0]).bitcast(I32), 0)
+        quantize(z_codes[:], z_scales[:], flat(u_bf[0]))
         for ab in range(2):
             nc.vector.memset(k_bf[ab][:].rearrange("p j z m t -> p (j z m t)").bitcast(I32), 0)
-        quantize(z_codes[:], z_scales[:], k_bf[0][:, 0:2].rearrange("p j z m t -> p (j z m t)"))
-        warm_up(z_codes[:], z_scales[:], 24)
+        warm_up(z_codes[:], z_scales[:], 20)
 
         deal_keys(0)
         interleave(nc.vector.tensor_copy, s_bf[0][:], s_raw[0][:])
         quantize_keys(0)
         warm_up(codes1[:, D : 2 * D], scales1[:, D : 2 * D], 4)
         quantize_state(0)
-        warm_up(codes1[:, 0:D], scales1[:, 0:D], 2)
+        warm_up(codes1[:, 0:D], scales1[:, 0:D], 4)
         deal_keys(1)
         interleave(nc.vector.tensor_copy, s_bf[1][:], s_raw[1][:])
         quantize_keys(1)
@@ -239,7 +239,7 @@ def tile_rows_upd_titans_kernel(tc, kT, S, v, be, kn, mo, out):
         quantize_state(1)
         first_product((0, 2))
         first_product((1, 3))
-        warm_up(z_codes[:], z_scales[:], 18)
+        warm_up(z_codes[:], z_scales[:], 10)
 
         interleave(nc.scalar.copy, n_bf[0][:], n_raw[:, 0])
         interleave(nc.vector.tensor_copy, n_bf[1][:], n_raw[:, 1])
@@ -273,6 +273,6 @@ def tile_rows_upd_titans_kernel(tc, kT, S, v, be, kn, mo, out):
         finish(1, (1, 3))
         store(nc.sync, 1, 2, 4)
         finish(1, (0,))
-        store(nc.scalar, 1, 0, 1)
+        store(nc.sync, 1, 0, 1)
         finish(1, (2,))
         store(nc.sync, 1, 1, 2)

@@ -17,7 +17,18 @@ ACT = mybir.ActivationFunctionType
 P = 128
 R = 32
 PACK = 4
+TILES = P // R
+LOW, HIGH = 0, 1
 FIRST_HEAD = (0, 4, 2, 6)
+STATE_DECAY, MOMENTUM_DECAY = 0.95, 0.9
+
+STATE_AT = (0, 5 * D)
+KEYS_AT = (D, 3 * D)
+STEP_COLUMNS = 2 * R
+
+EARLY = ((0, 0), (2, 0), (0, 2), (1, 0), (3, 0), (1, 2), (3, 2))
+
+WARM_START, WARM_KEYS, WARM_STATE, WARM_BETWEEN = 20, 4, 4, 10
 
 
 def tile_rows_upd_titans_kernel(tc, kT, S, v, be, kn, mo, out):
@@ -47,22 +58,85 @@ def tile_rows_upd_titans_kernel(tc, kT, S, v, be, kn, mo, out):
         u_scales = pair("u_scales", [P, D], U8)
         n_codes = pair("n_codes", [P, D], U32)
         n_scales = pair("n_scales", [P, D], U8)
-        s_nat = pair("s_nat", [P, 4, D], F32)
-        m_nat = pair("m_nat", [P, 4, D], F32)
-        acc = pair("acc", [P, 4, D], F32)
-        res = pair("res", [P, 4, D], F32)
-        warm = sb.tile([P, 8], F32, name="warm")
-        warm_out = sb.tile([P, 8], F32, name="warm_out")
-        z_codes = sb.tile([P, D], U32, name="z_codes", align_bytes=64)
-        z_scales = sb.tile([P, D], U8, name="z_scales", align_bytes=64)
-        banks = [ps.tile([P, 4, D], F32, name=f"bank{i}") for i in range(8)]
+        s_nat = pair("s_nat", [P, TILES, D], F32)
+        m_nat = pair("m_nat", [P, TILES, D], F32)
+        acc = pair("acc", [P, TILES, D], F32)
+        res = pair("res", [P, TILES, D], F32)
+        table_in = sb.tile([P, 8], F32, name="table_in")
+        table_out = sb.tile([P, 8], F32, name="table_out")
+        zero_codes = sb.tile([P, D], U32, name="zero_codes", align_bytes=64)
+        zero_scales = sb.tile([P, D], U8, name="zero_scales", align_bytes=64)
+
+        banks = [ps.tile([P, PACK, D], F32, name=f"bank{i}") for i in range(8)]
         bank = [[banks[0], banks[1]], [banks[2], banks[3]], [banks[4], banks[4]], [banks[5], banks[6]]]
         warm_bank = banks[7]
 
-        def warm_up(codes, scales, n):
-            for i in range(n):
+        def quadrant(q):
+            return slice(R * q, R * q + R)
+
+        def flat(tile):
+            return tile[:].rearrange("p c t -> p (c t)")
+
+        def flat_keys(half):
+            return k_bf[half][:].rearrange("p j z m t -> p (j z m t)")
+
+        def by_set(tensor, s):
+            return tensor.rearrange("(k s) f e -> s f k e", s=2)[s]
+
+        def load_heads(dst, src, half):
+            rows = src[TILES * half : TILES * half + TILES].rearrange("g (p t) c -> (g p) t c", t=PACK)
+            nc.sync.dma_start(out=dst[half][:], in_=rows)
+
+        def load_quadrant(dst, src, q):
+            head = FIRST_HEAD[q]
+            nc.sync.dma_start(
+                out=dst[quadrant(q)].rearrange("p s t c -> p s (t c)"),
+                in_=src[head : head + 2].rearrange("s (p t) c -> p s (t c)", t=PACK),
+            )
+
+        def load_steps(q):
+            head = FIRST_HEAD[q]
+            nc.scalar.dma_start(
+                out=be_sb[quadrant(q), :, 0:PACK],
+                in_=be[head : head + 2].rearrange("s (p j) o -> p s (j o)", j=PACK),
+            )
+
+        def in_words(ap):
+            return ap.rearrange("p (c i) t -> p c t i", i=4)
+
+        def in_rows(ap):
+            return ap.rearrange("p t (c i) -> p c t i", i=4)
+
+        def interleave(copy, dst, src):
+            copy(out=in_words(dst), in_=in_rows(src))
+
+        def deal_keys(half):
+            nc.scalar.copy(
+                out=k_bf[half][:, :, half, :, :].rearrange("p j m t -> p m j t"),
+                in_=k_raw[half][:].rearrange("p t (m j) -> p m j t", j=PACK),
+            )
+
+        def quantize(codes, scales, src):
+            nc.vector.quantize_mx(out=codes.bitcast(FP8X4), scales=scales, in_=src)
+
+        def quantize_keys(half):
+            cols = slice(KEYS_AT[half], KEYS_AT[half] + 2 * D)
+            quantize(codes1[:, cols], scales1[:, cols], flat_keys(half))
+
+        def quantize_state(half):
+            cols = slice(STATE_AT[half], STATE_AT[half] + D)
+            quantize(codes1[:, cols], scales1[:, cols], flat(s_bf[half]))
+
+        def quantize_u(s):
+            quantize(u_codes[s][:], u_scales[s][:], flat(u_bf[s]))
+
+        def quantize_kn(s):
+            quantize(n_codes[s][:], n_scales[s][:], flat(n_bf[s]))
+
+        def warm_up(codes, scales, count):
+            for i in range(count):
                 nc.tensor.matmul_mx(
-                    out=warm_bank[:, i % 4, :],
+                    out=warm_bank[:, i % PACK, :],
                     lhsT=codes.bitcast(FP8X4),
                     lhsT_scale=scales,
                     rhs=codes.bitcast(FP8X4),
@@ -71,129 +145,48 @@ def tile_rows_upd_titans_kernel(tc, kT, S, v, be, kn, mo, out):
                     stop=True,
                 )
 
-
-        S_AT = (0, 5 * D)
-        K_AT = (D, 3 * D)
-
-        def load_rows(eng, dst, src, ab):
-            eng.dma_start(out=dst[ab][:], in_=src[4 * ab : 4 * ab + 4].rearrange("g (p t) c -> (g p) t c", t=PACK))
-
-        def load_quad(eng, dst, src, q):
-            h = FIRST_HEAD[q]
-            eng.dma_start(
-                out=dst[R * q : R * q + R].rearrange("p s t c -> p s (t c)"),
-                in_=src[h : h + 2].rearrange("s (p t) c -> p s (t c)", t=PACK),
+        def z_pass(r, j, half):
+            first = KEYS_AT[half] + STEP_COLUMNS * (j - r // 2)
+            window = slice(first, first + D)
+            state = slice(STATE_AT[half], STATE_AT[half] + D)
+            nc.tensor.matmul_mx(
+                out=bank[r][j // 2][:, j, :],
+                lhsT=codes1[quadrant(r), window].bitcast(FP8X4),
+                lhsT_scale=scales1[quadrant(r), window],
+                rhs=codes1[quadrant(r), state].bitcast(FP8X4),
+                rhs_scale=scales1[quadrant(r), state],
+                start=(half == LOW),
+                stop=(half == HIGH),
             )
 
-        def nat(src, s):
-            return src.rearrange("(k s) f e -> s f k e", s=2)[s]
+        def first_product(s):
+            for j in range(PACK):
+                for half in (LOW, HIGH):
+                    for r in (s, s + 2):
+                        if half == HIGH or (r, j) not in EARLY:
+                            z_pass(r, j, half)
 
-        def interleave(copy, dst, src):
-            copy(out=dst.rearrange("p (c i) t -> p c t i", i=4), in_=src.rearrange("p t (c i) -> p c t i", i=4))
+        def z_rows(r):
+            return slice(2 * R * (r // 2), 2 * R * (r // 2) + 2 * R)
 
-        def deal_keys(ab):
-            nc.scalar.copy(
-                out=k_bf[ab][:, :, ab, :, :].rearrange("p j m t -> p m j t"),
-                in_=k_raw[ab][:].rearrange("p t (m j) -> p m j t", j=PACK),
-            )
-
-        def quantize(codes, scales, src):
-            nc.vector.quantize_mx(out=codes.bitcast(FP8X4), scales=scales, in_=src)
-
-        def quantize_keys(ab):
-            cols = slice(K_AT[ab], K_AT[ab] + 2 * D)
-            quantize(codes1[:, cols], scales1[:, cols], k_bf[ab][:].rearrange("p j z m t -> p (j z m t)"))
-
-        def quantize_state(ab):
-            cols = slice(S_AT[ab], S_AT[ab] + D)
-            quantize(codes1[:, cols], scales1[:, cols], s_bf[ab][:].rearrange("p c t -> p (c t)"))
-
-        def useful(r):
-            return slice(64 * (r // 2), 64 * (r // 2) + 64)
-
-        def scale_z_scalar(r, h):
-            rows = useful(r)
-            for jj in range(2):
-                j = 2 * h + jj
+        def scale_z_on_scalar(r, j0, j1):
+            rows = z_rows(r)
+            for j in range(j0, j1):
                 nc.scalar.activation(
-                    out=zb[r % 2][rows, j, :], in_=bank[r][h][rows, j, :], func=ACT.Copy, scale=be_sb[rows, r % 2, j : j + 1]
+                    out=zb[r % 2][rows, j, :],
+                    in_=bank[r][j // 2][rows, j, :],
+                    func=ACT.Copy,
+                    scale=be_sb[rows, r % 2, j : j + 1],
                 )
 
-        def scale_z_vector(r, j0, j1):
-            rows = useful(r)
+        def scale_z_on_vector(r, j0, j1):
+            rows = z_rows(r)
             nc.vector.tensor_tensor(
                 out=zb[r % 2][rows, j0:j1, :],
                 in0=bank[r][j0 // 2][rows, j0:j1, :],
-                in1=be_sb[rows, r % 2, j0:j1].unsqueeze(2).to_broadcast([64, j1 - j0, D]),
+                in1=be_sb[rows, r % 2, j0:j1].unsqueeze(2).to_broadcast([2 * R, j1 - j0, D]),
                 op=ALU.mult,
             )
-
-        def make_u(s):
-            nc.vector.tensor_tensor(
-                out=u_bf[s][:].rearrange("p (c i) j -> p c j i", i=4),
-                in0=vb[s][:].rearrange("p j (c i) -> p c j i", i=4),
-                in1=zb[s][:].rearrange("p j (c i) -> p c j i", i=4),
-                op=ALU.subtract,
-            )
-
-        def second_product(s):
-            for q in ((2, 0, 1, 3), (1, 3, 0, 2))[s]:
-                rows = slice(R * q, R * q + R)
-                nc.tensor.matmul_mx(
-                    out=bank[q][s][:, s, :],
-                    lhsT=n_codes[s][rows, :].bitcast(FP8X4),
-                    lhsT_scale=n_scales[s][rows, :],
-                    rhs=u_codes[s][rows, :].bitcast(FP8X4),
-                    rhs_scale=u_scales[s][rows, :],
-                    start=True,
-                    stop=True,
-                )
-
-        def make_base(s, half):
-            ks = slice(2 * half, 2 * half + 2)
-            nc.vector.scalar_tensor_tensor(
-                out=acc[s][:, ks, :], in0=s_nat[s][:, ks, :], scalar=0.95 / 0.9, in1=m_nat[s][:, ks, :], op0=ALU.mult, op1=ALU.add
-            )
-
-        def finish(s, qs):
-            for q in qs:
-                k = FIRST_HEAD[q] // 2
-                nc.vector.scalar_tensor_tensor(
-                    out=res[s][:, k, :], in0=acc[s][:, k, :], scalar=0.9, in1=bank[q][s][:, s, :], op0=ALU.mult, op1=ALU.add
-                )
-
-        def store(eng, s, k0, k1):
-            eng.dma_start(out=nat(out, s)[:, k0:k1, :], in_=res[s][:, k0:k1, :])
-
-        def scale_v_scalar(s):
-            for j in range(PACK):
-                nc.scalar.activation(out=vb[s][:, j, :], in_=v_raw[:, s, j, :], func=ACT.Copy, scale=be_sb[:, s, j : j + 1])
-
-        def load_steps(eng, q):
-            h = FIRST_HEAD[q]
-            eng.dma_start(out=be_sb[R * q : R * q + R, :, 0:PACK], in_=be[h : h + 2].rearrange("s (p j) o -> p s (j o)", j=PACK))
-
-        def z_pass(r, j, ab):
-            rows = slice(R * r, R * r + R)
-            c0 = K_AT[ab] + 64 * j - 64 * (r // 2)
-            nc.tensor.matmul_mx(
-                out=bank[r][j // 2][:, j, :],
-                lhsT=codes1[rows, c0 : c0 + D].bitcast(FP8X4),
-                lhsT_scale=scales1[rows, c0 : c0 + D],
-                rhs=codes1[rows, S_AT[ab] : S_AT[ab] + D].bitcast(FP8X4),
-                rhs_scale=scales1[rows, S_AT[ab] : S_AT[ab] + D],
-                start=(ab == 0),
-                stop=(ab == 1),
-            )
-
-        early = [(0, 0), (2, 0), (0, 2), (1, 0), (3, 0), (1, 2), (3, 2)]
-
-        def first_product(tiles):
-            for j in range(PACK):
-                for ab in range(2):
-                    for r in tiles:
-                        if ab == 1 or (r, j) not in early:
-                            z_pass(r, j, ab)
 
         def scale_v(s):
             for j in range(PACK):
@@ -201,78 +194,111 @@ def tile_rows_upd_titans_kernel(tc, kT, S, v, be, kn, mo, out):
                     out=vb[s][:, j, :], in0=v_raw[:, s, j, :], scalar1=be_sb[:, s, j : j + 1], scalar2=None, op0=ALU.mult
                 )
 
-        def flat(t):
-            return t[:].rearrange("p c t -> p (c t)")
+        def make_u(s):
+            nc.vector.tensor_tensor(out=in_words(u_bf[s][:]), in0=in_rows(vb[s][:]), in1=in_rows(zb[s][:]), op=ALU.subtract)
 
-        load_rows(nc.sync, k_raw, kT, 0)
-        for q in range(4):
-            load_steps(nc.scalar, q)
-        load_rows(nc.sync, s_raw, S, 0)
-        load_rows(nc.sync, k_raw, kT, 1)
-        load_rows(nc.sync, s_raw, S, 1)
-        for dst, src in ((n_raw, kn), (v_raw, v)):
+        def second_product(s, quadrants):
+            for q in quadrants:
+                nc.tensor.matmul_mx(
+                    out=bank[q][s][:, s, :],
+                    lhsT=n_codes[s][quadrant(q), :].bitcast(FP8X4),
+                    lhsT_scale=n_scales[s][quadrant(q), :],
+                    rhs=u_codes[s][quadrant(q), :].bitcast(FP8X4),
+                    rhs_scale=u_scales[s][quadrant(q), :],
+                    start=True,
+                    stop=True,
+                )
+
+        def scaled_add(dst, src, factor, other):
+            nc.vector.scalar_tensor_tensor(out=dst, in0=src, scalar=factor, in1=other, op0=ALU.mult, op1=ALU.add)
+
+        def store(s, k0, k1):
+            nc.sync.dma_start(out=by_set(out, s)[:, k0:k1, :], in_=res[s][:, k0:k1, :])
+
+        def join_set0(k0, k1):
+            scaled_add(acc[0][:, k0:k1, :], s_nat[0][:, k0:k1, :], STATE_DECAY / MOMENTUM_DECAY, m_nat[0][:, k0:k1, :])
+
+        def finish_set0(quadrants):
+            for q in quadrants:
+                k = FIRST_HEAD[q] // 2
+                scaled_add(res[0][:, k, :], acc[0][:, k, :], MOMENTUM_DECAY, bank[q][0][:, 0, :])
+
+        def join_set1(quadrants):
+            for q in quadrants:
+                k = FIRST_HEAD[q] // 2
+                scaled_add(acc[1][:, k, :], s_nat[1][:, k, :], STATE_DECAY, bank[q][1][:, 1, :])
+
+        def finish_set1(k0, k1):
+            scaled_add(res[1][:, k0:k1, :], m_nat[1][:, k0:k1, :], MOMENTUM_DECAY, acc[1][:, k0:k1, :])
+
+        load_heads(k_raw, kT, LOW)
+        for q in range(TILES):
+            load_steps(q)
+        load_heads(s_raw, S, LOW)
+        load_heads(k_raw, kT, HIGH)
+        load_heads(s_raw, S, HIGH)
+        for dst, src in ((v_raw, v), (n_raw, kn)):
             for q in (0, 2, 1, 3):
-                load_quad(nc.sync, dst, src, q)
-        for s in range(2):
-            nc.sync.dma_start(out=s_nat[s][:], in_=nat(S, s))
-            nc.sync.dma_start(out=m_nat[s][:], in_=nat(mo, s))
+                load_quadrant(dst, src, q)
+        nc.sync.dma_start(out=s_nat[0][:], in_=by_set(S, 0))
+        nc.sync.dma_start(out=m_nat[0][:], in_=by_set(mo, 0))
+        nc.sync.dma_start(out=s_nat[1][:], in_=by_set(S, 1))
+        for k0 in (2, 0):
+            nc.sync.dma_start(out=m_nat[1][:, k0 : k0 + 2, :], in_=by_set(mo, 1)[:, k0 : k0 + 2, :])
 
-        nc.vector.memset(warm[:], 0.0)
-        nc.scalar.activation(out=warm_out[:], in_=warm[:], func=ACT.Copy, scale=warm[:, 0:1])
+        nc.vector.memset(table_in[:], 0.0)
+        nc.scalar.activation(out=table_out[:], in_=table_in[:], func=ACT.Copy, scale=table_in[:, 0:1])
         nc.vector.memset(flat(u_bf[0]).bitcast(I32), 0)
-        quantize(z_codes[:], z_scales[:], flat(u_bf[0]))
-        for ab in range(2):
-            nc.vector.memset(k_bf[ab][:].rearrange("p j z m t -> p (j z m t)").bitcast(I32), 0)
-        warm_up(z_codes[:], z_scales[:], 20)
+        quantize(zero_codes[:], zero_scales[:], flat(u_bf[0]))
+        for half in (LOW, HIGH):
+            nc.vector.memset(flat_keys(half).bitcast(I32), 0)
+        warm_up(zero_codes[:], zero_scales[:], WARM_START)
 
-        deal_keys(0)
-        interleave(nc.vector.tensor_copy, s_bf[0][:], s_raw[0][:])
-        quantize_keys(0)
-        warm_up(codes1[:, D : 2 * D], scales1[:, D : 2 * D], 4)
-        quantize_state(0)
-        warm_up(codes1[:, 0:D], scales1[:, 0:D], 4)
-        deal_keys(1)
-        interleave(nc.vector.tensor_copy, s_bf[1][:], s_raw[1][:])
-        quantize_keys(1)
-        for r, j in early:
-            z_pass(r, j, 0)
-        quantize_state(1)
-        first_product((0, 2))
-        first_product((1, 3))
-        warm_up(z_codes[:], z_scales[:], 10)
+        deal_keys(LOW)
+        interleave(nc.vector.tensor_copy, s_bf[LOW][:], s_raw[LOW][:])
+        quantize_keys(LOW)
+        warm_up(codes1[:, D : 2 * D], scales1[:, D : 2 * D], WARM_KEYS)
+        quantize_state(LOW)
+        warm_up(codes1[:, 0:D], scales1[:, 0:D], WARM_STATE)
+        deal_keys(HIGH)
+        interleave(nc.vector.tensor_copy, s_bf[HIGH][:], s_raw[HIGH][:])
+        quantize_keys(HIGH)
+        for r, j in EARLY:
+            z_pass(r, j, LOW)
+        quantize_state(HIGH)
+        first_product(0)
+        first_product(1)
+        warm_up(zero_codes[:], zero_scales[:], WARM_BETWEEN)
 
-        interleave(nc.scalar.copy, n_bf[0][:], n_raw[:, 0])
-        interleave(nc.vector.tensor_copy, n_bf[1][:], n_raw[:, 1])
-        quantize(n_codes[1][:], n_scales[1][:], flat(n_bf[1]))
-        quantize(n_codes[0][:], n_scales[0][:], flat(n_bf[0]))
-
-        scale_z_scalar(0, 0)
-        scale_z_scalar(0, 1)
-        scale_z_vector(2, 0, 4)
         scale_v(0)
         scale_v(1)
-        scale_z_scalar(1, 0)
-        scale_z_scalar(3, 0)
+        scale_z_on_scalar(0, 0, 4)
+        scale_z_on_scalar(1, 0, 2)
+        scale_z_on_vector(2, 0, 4)
+        scale_z_on_vector(3, 0, 2)
         make_u(0)
-        scale_z_scalar(1, 1)
-        scale_z_scalar(3, 1)
-        make_base(0, 0)
-        quantize(u_codes[0][:], u_scales[0][:], flat(u_bf[0]))
+        scale_z_on_scalar(1, 2, 4)
+        scale_z_on_scalar(3, 2, 4)
+        interleave(nc.vector.tensor_copy, n_bf[0][:], n_raw[:, 0])
+        quantize_u(0)
         make_u(1)
-        second_product(0)
-        make_base(0, 1)
-        quantize(u_codes[1][:], u_scales[1][:], flat(u_bf[1]))
-        finish(0, (2,))
-        second_product(1)
-        finish(0, (0,))
-        store(nc.sync, 0, 0, 2)
-        finish(0, (1, 3))
-        store(nc.sync, 0, 2, 4)
-        make_base(1, 1)
-        make_base(1, 0)
-        finish(1, (1, 3))
-        store(nc.sync, 1, 2, 4)
-        finish(1, (0,))
-        store(nc.sync, 1, 0, 1)
-        finish(1, (2,))
-        store(nc.sync, 1, 1, 2)
+        interleave(nc.scalar.copy, n_bf[1][:], n_raw[:, 1])
+        quantize_kn(0)
+        second_product(0, (2, 0, 1, 3))
+        quantize_kn(1)
+        quantize_u(1)
+
+        join_set0(0, 2)
+        join_set0(2, 4)
+        finish_set0((2, 0))
+        store(0, 0, 2)
+        second_product(1, (1, 3, 0, 2))
+        join_set1((1, 3))
+        finish_set0((1, 3))
+        store(0, 2, 4)
+        finish_set1(2, 4)
+        store(1, 2, 4)
+        join_set1((0, 2))
+        for k in range(2):
+            finish_set1(k, k + 1)
+            store(1, k, k + 1)

from contextlib import ExitStack

import concourse.mybir as mybir

G, D = 8, 128
FLOPS = 2 * 2 * G * D * D * D

F32 = mybir.dt.float32
BF16 = mybir.dt.bfloat16
U32 = mybir.dt.uint32
I32 = mybir.dt.int32
U8 = mybir.dt.uint8
FP8X4 = mybir.dt.float8_e4m3fn_x4
ALU = mybir.AluOpType
ACT = mybir.ActivationFunctionType

P = 128
R = 32
PACK = 4
TILES = P // R
LOW, HIGH = 0, 1
FIRST_HEAD = (0, 4, 2, 6)
STATE_DECAY, MOMENTUM_DECAY = 0.95, 0.9

STATE_AT = (0, 5 * D)
KEYS_AT = (D, 3 * D)
STEP_COLUMNS = 2 * R

EARLY = ((0, 0), (2, 0), (0, 2), (1, 0), (3, 0), (1, 2), (3, 2))

WARM_START, WARM_KEYS, WARM_STATE, WARM_BETWEEN = 20, 4, 4, 10


def tile_rows_upd_titans_kernel(tc, kT, S, v, be, kn, mo, out):
    nc = tc.nc
    with ExitStack() as ctx:
        sb = ctx.enter_context(tc.tile_pool(name="sb", bufs=1))
        ps = ctx.enter_context(tc.psum_pool(name="ps", bufs=1))
        ctx.enter_context(tc.manual_schedule())

        def pair(name, shape, dtype):
            return [sb.tile(shape, dtype, name=f"{name}{i}", align_bytes=64) for i in range(2)]

        k_raw = pair("k_raw", [P, PACK, D], F32)
        s_raw = pair("s_raw", [P, PACK, D], F32)
        k_bf = pair("k_bf", [P, PACK, 2, R, PACK], BF16)
        s_bf = pair("s_bf", [P, D, PACK], BF16)
        codes1 = sb.tile([P, 6 * D], U32, name="codes1", align_bytes=64)
        scales1 = sb.tile([P, 6 * D], U8, name="scales1", align_bytes=64)
        v_raw = sb.tile([P, 2, PACK, D], F32, name="v_raw")
        n_raw = sb.tile([P, 2, PACK, D], F32, name="n_raw")
        be_sb = sb.tile([P, 2, 8], F32, name="be_sb")
        vb = pair("vb", [P, PACK, D], F32)
        zb = pair("zb", [P, PACK, D], F32)
        u_bf = pair("u_bf", [P, D, PACK], BF16)
        n_bf = pair("n_bf", [P, D, PACK], BF16)
        u_codes = pair("u_codes", [P, D], U32)
        u_scales = pair("u_scales", [P, D], U8)
        n_codes = pair("n_codes", [P, D], U32)
        n_scales = pair("n_scales", [P, D], U8)
        s_nat = pair("s_nat", [P, TILES, D], F32)
        m_nat = pair("m_nat", [P, TILES, D], F32)
        acc = pair("acc", [P, TILES, D], F32)
        res = pair("res", [P, TILES, D], F32)
        table_in = sb.tile([P, 8], F32, name="table_in")
        table_out = sb.tile([P, 8], F32, name="table_out")
        zero_codes = sb.tile([P, D], U32, name="zero_codes", align_bytes=64)
        zero_scales = sb.tile([P, D], U8, name="zero_scales", align_bytes=64)

        banks = [ps.tile([P, PACK, D], F32, name=f"bank{i}") for i in range(8)]
        bank = [[banks[0], banks[1]], [banks[2], banks[3]], [banks[4], banks[4]], [banks[5], banks[6]]]
        warm_bank = banks[7]

        def quadrant(q):
            return slice(R * q, R * q + R)

        def flat(tile):
            return tile[:].rearrange("p c t -> p (c t)")

        def flat_keys(half):
            return k_bf[half][:].rearrange("p j z m t -> p (j z m t)")

        def by_set(tensor, s):
            return tensor.rearrange("(k s) f e -> s f k e", s=2)[s]

        def load_heads(dst, src, half):
            rows = src[TILES * half : TILES * half + TILES].rearrange("g (p t) c -> (g p) t c", t=PACK)
            nc.sync.dma_start(out=dst[half][:], in_=rows)

        def load_quadrant(dst, src, q):
            head = FIRST_HEAD[q]
            nc.sync.dma_start(
                out=dst[quadrant(q)].rearrange("p s t c -> p s (t c)"),
                in_=src[head : head + 2].rearrange("s (p t) c -> p s (t c)", t=PACK),
            )

        def load_steps(q):
            head = FIRST_HEAD[q]
            nc.scalar.dma_start(
                out=be_sb[quadrant(q), :, 0:PACK],
                in_=be[head : head + 2].rearrange("s (p j) o -> p s (j o)", j=PACK),
            )

        def in_words(ap):
            return ap.rearrange("p (c i) t -> p c t i", i=4)

        def in_rows(ap):
            return ap.rearrange("p t (c i) -> p c t i", i=4)

        def interleave(copy, dst, src):
            copy(out=in_words(dst), in_=in_rows(src))

        def deal_keys(half):
            nc.scalar.copy(
                out=k_bf[half][:, :, half, :, :].rearrange("p j m t -> p m j t"),
                in_=k_raw[half][:].rearrange("p t (m j) -> p m j t", j=PACK),
            )

        def quantize(codes, scales, src):
            nc.vector.quantize_mx(out=codes.bitcast(FP8X4), scales=scales, in_=src)

        def quantize_keys(half):
            cols = slice(KEYS_AT[half], KEYS_AT[half] + 2 * D)
            quantize(codes1[:, cols], scales1[:, cols], flat_keys(half))

        def quantize_state(half):
            cols = slice(STATE_AT[half], STATE_AT[half] + D)
            quantize(codes1[:, cols], scales1[:, cols], flat(s_bf[half]))

        def quantize_u(s):
            quantize(u_codes[s][:], u_scales[s][:], flat(u_bf[s]))

        def quantize_kn(s):
            quantize(n_codes[s][:], n_scales[s][:], flat(n_bf[s]))

        def warm_up(codes, scales, count):
            for i in range(count):
                nc.tensor.matmul_mx(
                    out=warm_bank[:, i % PACK, :],
                    lhsT=codes.bitcast(FP8X4),
                    lhsT_scale=scales,
                    rhs=codes.bitcast(FP8X4),
                    rhs_scale=scales,
                    start=True,
                    stop=True,
                )

        def z_pass(r, j, half):
            first = KEYS_AT[half] + STEP_COLUMNS * (j - r // 2)
            window = slice(first, first + D)
            state = slice(STATE_AT[half], STATE_AT[half] + D)
            nc.tensor.matmul_mx(
                out=bank[r][j // 2][:, j, :],
                lhsT=codes1[quadrant(r), window].bitcast(FP8X4),
                lhsT_scale=scales1[quadrant(r), window],
                rhs=codes1[quadrant(r), state].bitcast(FP8X4),
                rhs_scale=scales1[quadrant(r), state],
                start=(half == LOW),
                stop=(half == HIGH),
            )

        def first_product(s):
            for j in range(PACK):
                for half in (LOW, HIGH):
                    for r in (s, s + 2):
                        if half == HIGH or (r, j) not in EARLY:
                            z_pass(r, j, half)

        def z_rows(r):
            return slice(2 * R * (r // 2), 2 * R * (r // 2) + 2 * R)

        def scale_z_on_scalar(r, j0, j1):
            rows = z_rows(r)
            for j in range(j0, j1):
                nc.scalar.activation(
                    out=zb[r % 2][rows, j, :],
                    in_=bank[r][j // 2][rows, j, :],
                    func=ACT.Copy,
                    scale=be_sb[rows, r % 2, j : j + 1],
                )

        def scale_z_on_vector(r, j0, j1):
            rows = z_rows(r)
            nc.vector.tensor_tensor(
                out=zb[r % 2][rows, j0:j1, :],
                in0=bank[r][j0 // 2][rows, j0:j1, :],
                in1=be_sb[rows, r % 2, j0:j1].unsqueeze(2).to_broadcast([2 * R, j1 - j0, D]),
                op=ALU.mult,
            )

        def scale_v(s):
            for j in range(PACK):
                nc.vector.tensor_scalar(
                    out=vb[s][:, j, :], in0=v_raw[:, s, j, :], scalar1=be_sb[:, s, j : j + 1], scalar2=None, op0=ALU.mult
                )

        def make_u(s):
            nc.vector.tensor_tensor(out=in_words(u_bf[s][:]), in0=in_rows(vb[s][:]), in1=in_rows(zb[s][:]), op=ALU.subtract)

        def second_product(s, quadrants):
            for q in quadrants:
                nc.tensor.matmul_mx(
                    out=bank[q][s][:, s, :],
                    lhsT=n_codes[s][quadrant(q), :].bitcast(FP8X4),
                    lhsT_scale=n_scales[s][quadrant(q), :],
                    rhs=u_codes[s][quadrant(q), :].bitcast(FP8X4),
                    rhs_scale=u_scales[s][quadrant(q), :],
                    start=True,
                    stop=True,
                )

        def scaled_add(dst, src, factor, other):
            nc.vector.scalar_tensor_tensor(out=dst, in0=src, scalar=factor, in1=other, op0=ALU.mult, op1=ALU.add)

        def store(s, k0, k1):
            nc.sync.dma_start(out=by_set(out, s)[:, k0:k1, :], in_=res[s][:, k0:k1, :])

        def join_set0(k0, k1):
            scaled_add(acc[0][:, k0:k1, :], s_nat[0][:, k0:k1, :], STATE_DECAY / MOMENTUM_DECAY, m_nat[0][:, k0:k1, :])

        def finish_set0(quadrants):
            for q in quadrants:
                k = FIRST_HEAD[q] // 2
                scaled_add(res[0][:, k, :], acc[0][:, k, :], MOMENTUM_DECAY, bank[q][0][:, 0, :])

        def join_set1(quadrants):
            for q in quadrants:
                k = FIRST_HEAD[q] // 2
                scaled_add(acc[1][:, k, :], s_nat[1][:, k, :], STATE_DECAY, bank[q][1][:, 1, :])

        def finish_set1(k0, k1):
            scaled_add(res[1][:, k0:k1, :], m_nat[1][:, k0:k1, :], MOMENTUM_DECAY, acc[1][:, k0:k1, :])

        load_heads(k_raw, kT, LOW)
        for q in range(TILES):
            load_steps(q)
        load_heads(s_raw, S, LOW)
        load_heads(k_raw, kT, HIGH)
        load_heads(s_raw, S, HIGH)
        for dst, src in ((v_raw, v), (n_raw, kn)):
            for q in (0, 2, 1, 3):
                load_quadrant(dst, src, q)
        nc.sync.dma_start(out=s_nat[0][:], in_=by_set(S, 0))
        nc.sync.dma_start(out=m_nat[0][:], in_=by_set(mo, 0))
        nc.sync.dma_start(out=s_nat[1][:], in_=by_set(S, 1))
        for k0 in (2, 0):
            nc.sync.dma_start(out=m_nat[1][:, k0 : k0 + 2, :], in_=by_set(mo, 1)[:, k0 : k0 + 2, :])

        nc.vector.memset(table_in[:], 0.0)
        nc.scalar.activation(out=table_out[:], in_=table_in[:], func=ACT.Copy, scale=table_in[:, 0:1])
        nc.vector.memset(flat(u_bf[0]).bitcast(I32), 0)
        quantize(zero_codes[:], zero_scales[:], flat(u_bf[0]))
        for half in (LOW, HIGH):
            nc.vector.memset(flat_keys(half).bitcast(I32), 0)
        warm_up(zero_codes[:], zero_scales[:], WARM_START)

        deal_keys(LOW)
        interleave(nc.vector.tensor_copy, s_bf[LOW][:], s_raw[LOW][:])
        quantize_keys(LOW)
        warm_up(codes1[:, D : 2 * D], scales1[:, D : 2 * D], WARM_KEYS)
        quantize_state(LOW)
        warm_up(codes1[:, 0:D], scales1[:, 0:D], WARM_STATE)
        deal_keys(HIGH)
        interleave(nc.vector.tensor_copy, s_bf[HIGH][:], s_raw[HIGH][:])
        quantize_keys(HIGH)
        for r, j in EARLY:
            z_pass(r, j, LOW)
        quantize_state(HIGH)
        first_product(0)
        first_product(1)
        warm_up(zero_codes[:], zero_scales[:], WARM_BETWEEN)

        scale_v(0)
        scale_v(1)
        scale_z_on_scalar(0, 0, 4)
        scale_z_on_scalar(1, 0, 2)
        scale_z_on_vector(2, 0, 4)
        scale_z_on_vector(3, 0, 2)
        make_u(0)
        scale_z_on_scalar(1, 2, 4)
        scale_z_on_scalar(3, 2, 4)
        interleave(nc.vector.tensor_copy, n_bf[0][:], n_raw[:, 0])
        quantize_u(0)
        make_u(1)
        interleave(nc.scalar.copy, n_bf[1][:], n_raw[:, 1])
        quantize_kn(0)
        second_product(0, (2, 0, 1, 3))
        quantize_kn(1)
        quantize_u(1)

        join_set0(0, 2)
        join_set0(2, 4)
        finish_set0((2, 0))
        store(0, 0, 2)
        second_product(1, (1, 3, 0, 2))
        join_set1((1, 3))
        finish_set0((1, 3))
        store(0, 2, 4)
        finish_set1(2, 4)
        store(1, 2, 4)
        join_set1((0, 2))
        for k in range(2):
            finish_set1(k, k + 1)
            store(1, k, k + 1)
